import numpy as np
import ml_dtypes


def mxq(x, axis, fmt="e4m3"):
    dtype, down = {"e4m3": (ml_dtypes.float8_e4m3fn, 7), "e5m2": (ml_dtypes.float8_e5m2, 14)}[fmt]
    v = np.moveaxis(np.asarray(x, np.float32).astype(ml_dtypes.bfloat16).astype(np.float64), axis, -1)
    blocks = v.reshape(v.shape[:-1] + (-1, 32))
    amax = np.abs(blocks).max(-1, keepdims=True)
    byte = np.maximum(np.where(amax > 0, np.frexp(amax)[1] - 1 + 127, 0) - down, 1)
    scale = np.exp2(byte - 127.0)
    codes = (blocks / scale).astype(np.float32).astype(dtype).astype(np.float64)
    return np.moveaxis((codes * scale).reshape(v.shape), -1, axis)


WIDE = False


def mx_kscale(k):
    if not WIDE:
        return np.ones(k)
    levels = np.array([10, -10, 5, -5, 0])
    if k % 512:
        return np.exp2(np.random.permutation(np.resize(levels, k // 32))).repeat(32)
    a = np.empty((k // 512, 16))
    for p in range(k // 512):
        a[p, :8] = np.random.permutation(np.resize(levels, 8))
        for g in range(8):
            far = levels[np.abs(levels - a[p, g]) >= 10]
            a[p, g + 8] = far[np.random.randint(len(far))]
    return np.exp2(a.ravel()).repeat(32)


def f64(x):
    return np.asarray(x).astype(np.float64)


def striped8(idx):
    return np.asarray(idx).reshape(8, -1, 16).transpose(0, 2, 1).reshape(128, -1).astype(np.uint16)


def unstriped8(offs):
    return offs.reshape(8, 16, -1).transpose(0, 2, 1).reshape(8, -1).astype(np.int64)


def pick8(x, idx, run):
    r = np.arange(len(x))
    return x[r[:, None], idx[r % (8 * run) // run]]


E2M1 = np.array([0.0, 0.5, 1.0, 1.5, 2.0, 3.0, 4.0, 6.0, -0.0, -0.5, -1.0, -1.5, -2.0, -3.0, -4.0, -6.0])


def pack_weight(w, fmt):
    k, n = w.shape
    w = f64(np.asarray(w, np.float32).astype(ml_dtypes.bfloat16)).reshape(k // 32, 32, n)
    amax = np.abs(w).max(1)
    if fmt == "e4m3":
        byte = np.frexp(amax)[1] - 1 + 127 - 7
    else:
        mant, ex = np.frexp(amax / 6.0)
        byte = np.where(mant > 0.5, ex, ex - 1) + 127
    byte = np.clip(np.where(amax > 0, byte, 1), 1, 254)
    scaled = (w * np.exp2(127.0 - byte)[:, None, :]).reshape(k, n).astype(np.float32)
    by_word = np.ascontiguousarray(scaled.reshape(k // 512, 128, 4, n).transpose(0, 1, 3, 2))
    if fmt == "e4m3":
        words = by_word.astype(ml_dtypes.float8_e4m3fn).view(np.uint8)
    else:
        c = by_word.astype(ml_dtypes.float4_e2m1fn).view(np.uint8) & 0xF
        words = (c[..., 0::2] | (c[..., 1::2] << 4)).reshape(k // 512, 128, 2 * n)
    return np.ascontiguousarray(words), np.ascontiguousarray(byte.astype(np.uint8).reshape(k // 512, 16, n))


def unpack_weight(words, scales, fmt):
    g, _, n = scales.shape
    words = np.ascontiguousarray(words).reshape(g, 128, n, -1)
    if fmt == "e4m3":
        vals = words.view(ml_dtypes.float8_e4m3fn).astype(np.float64)
    else:
        nib = np.empty((g, 128, n, 4), np.uint8)
        nib[..., 0::2] = words & 0xF
        nib[..., 1::2] = words >> 4
        vals = E2M1[nib]
    vals = vals * np.repeat(np.exp2(scales.astype(np.float64) - 127.0), 8, axis=1)[..., None]
    return vals.transpose(0, 1, 3, 2).reshape(g * 512, n)


D, K, T, U, Z, I, Q = 512, 512, 1024, 1024, 1024, 512, 128


def setup_inputs():
    n = np.random.standard_normal
    idx = np.stack([np.random.permutation(T)[:I] for _ in range(8)])
    idx2 = np.stack([np.random.permutation(U)[:I] for _ in range(8)])
    idx3 = np.stack([np.random.permutation(Z)[:I] for _ in range(8)])
    idx4 = np.stack([np.random.permutation(Z)[:I] for _ in range(8)])
    idx5 = np.stack([np.random.permutation(T)[:I] for _ in range(8)])
    fd = mx_kscale(D)
    fk = mx_kscale(K)
    wqp = pack_weight(n((D, K)) * 1.0 / np.sqrt(D) * fd[:, None] * fk, "e4m3")
    keysp = pack_weight(n((K, T)) * 1.0 / np.sqrt(K) / fk[:, None], "e4m3")
    notesp = pack_weight(n((D, U)) * 1.0 / np.sqrt(D) * fd[:, None], "e2m1")
    return {
        "states": (n((D, Q)) * 0.95 / fd[:, None]).astype(np.float32),
        "wq_words": wqp[0],
        "wq_scales": wqp[1],
        "keys_words": keysp[0],
        "keys_scales": keysp[1],
        "notes_words": notesp[0],
        "notes_scales": notesp[1],
        "offs": striped8(idx),
        "offs2": striped8(idx2),
        "offs3": striped8(idx3),
        "offs4": striped8(idx4),
        "offs5": striped8(idx5),
    }


def reference(states, wq_words, wq_scales, keys_words, keys_scales, notes_words, notes_scales, offs, offs2, offs3, offs4, offs5):
    idx = unstriped8(offs)
    idx2 = unstriped8(offs2)
    idx3 = unstriped8(offs3)
    idx4 = unstriped8(offs4)
    idx5 = unstriped8(offs5)
    wqu = unpack_weight(wq_words, wq_scales, "e4m3")
    keysu = unpack_weight(keys_words, keys_scales, "e4m3")
    notesu = unpack_weight(notes_words, notes_scales, "e2m1")
    statesq = mxq(f64(states), 0, "e4m3")
    qv = wqu.T @ statesq
    qvq = mxq(qv, 0, "e4m3")
    a = qvq.T @ keysu
    b = statesq.T @ notesu
    f1 = np.zeros((Q, Z))
    f1[np.arange(Q)[:, None], idx3[np.arange(Q) % 128 // 16]] = pick8(a, idx, 16)
    f2 = np.zeros((Q, Z))
    f2[np.arange(Q)[:, None], idx4[np.arange(Q) % 128 // 16]] = pick8(b, idx2, 16)
    m1 = np.maximum(f1, f2)
    w = pick8(m1, idx4, 16) - pick8(m1, idx3, 16)
    f3 = np.zeros((Q, T))
    f3[np.arange(Q)[:, None], idx5[np.arange(Q) % 128 // 16]] = w
    aa = a + f3
    y = pick8(aa, idx, 16)
    return y

@@ -1,0 +1,184 @@
+from contextlib import ExitStack
+
+import concourse.mybir as mybir
+
+D, K, T, U, Z, I, Q = 512, 512, 1024, 1024, 1024, 512, 128
+FLOPS = 2 * Q * (D * K + K * T + D * U)
+
+F32 = mybir.dt.float32
+BF16 = mybir.dt.bfloat16
+I32 = mybir.dt.int32
+U32 = mybir.dt.uint32
+U16 = mybir.dt.uint16
+U8 = mybir.dt.uint8
+FP8X4 = mybir.dt.float8_e4m3fn_x4
+FP4X4 = mybir.dt.float4_e2m1fn_x4
+ADD = mybir.AluOpType.add
+MULT = mybir.AluOpType.mult
+MAX = mybir.AluOpType.max
+COPY = mybir.ActivationFunctionType.Copy
+
+P = 128
+PACK = 4
+BANK = 512
+HALF = I // 2
+LIST_ROWS = 16
+
+
+def load_scale_rows(queue, plane, scales, quadrant):
+    queue.dma_start(
+        out=plane[32 * quadrant : 32 * quadrant + 4, :].bitcast(I32),
+        in_=scales[0, 4 * quadrant : 4 * quadrant + 4, :].bitcast(I32),
+    )
+
+
+def tile_attend_meetinghall_madeside_kernel(
+    tc, states, wq_words, wq_scales, keys_words, keys_scales, notes_words, notes_scales,
+    offs, offs2, offs3, offs4, offs5, out,
+):
+    nc = tc.nc
+    with ExitStack() as ctx:
+        sb = ctx.enter_context(tc.tile_pool(name="sb", bufs=1))
+        ps = ctx.enter_context(tc.psum_pool(name="ps", bufs=1))
+
+        def half(lists, h):
+            cols = HALF // LIST_ROWS
+            return lists[:, h * cols : (h + 1) * cols]
+
+        def slots(h):
+            return slice(h * HALF, (h + 1) * HALF)
+
+        idx = sb.tile([P, I // LIST_ROWS], U16, name="idx")
+        idx2 = sb.tile([P, I // LIST_ROWS], U16, name="idx2")
+        idx3 = sb.tile([P, I // LIST_ROWS], U16, name="idx3")
+        idx4 = sb.tile([P, I // LIST_ROWS], U16, name="idx4")
+        idx5 = sb.tile([P, I // LIST_ROWS], U16, name="idx5")
+
+        notes_plane = sb.tile([P, U], U8, name="notes_plane", align_bytes=64)
+        wq_plane = sb.tile([P, K], U8, name="wq_plane", align_bytes=64)
+        keys_plane = sb.tile([P, T], U8, name="keys_plane", align_bytes=64)
+        for plane in (notes_plane, wq_plane, keys_plane):
+            nc.vector.memset(plane[:].bitcast(I32), 0)
+        f1 = sb.tile([P, Z], F32, name="f1")
+        f2 = sb.tile([P, Z], F32, name="f2")
+        f3 = sb.tile([P, T], F32, name="f3")
+
+        states_raw = sb.tile([P, PACK, Q], F32, name="states_raw")
+        notes_codes = sb.tile([P, 2 * U], U8, name="notes_codes", align_bytes=64)
+        wq_codes = sb.tile([P, K], U32, name="wq_codes", align_bytes=64)
+        keys_codes = sb.tile([P, T], U32, name="keys_codes", align_bytes=64)
+
+        nc.sync.dma_start(out=states_raw[:], in_=states.rearrange("(p t) q -> p t q", t=PACK))
+        nc.scalar.dma_start(out=notes_codes[:].bitcast(I32), in_=notes_words[0].bitcast(I32))
+        for quadrant in range(4):
+            load_scale_rows(nc.sync, notes_plane, notes_scales, quadrant)
+        nc.scalar.dma_start(
+            out=wq_codes[:].bitcast(I32), in_=wq_words[0].rearrange("p k t -> p (k t)").bitcast(I32)
+        )
+        load_scale_rows(nc.sync, wq_plane, wq_scales, 0)
+        for quadrant in range(1, 4):
+            load_scale_rows(nc.gpsimd, wq_plane, wq_scales, quadrant)
+        nc.sync.dma_start(idx2[:], offs2)
+        nc.sync.dma_start(
+            out=keys_codes[:].bitcast(I32), in_=keys_words[0].rearrange("p n t -> p (n t)").bitcast(I32)
+        )
+        for quadrant in range(4):
+            load_scale_rows(nc.sync, keys_plane, keys_scales, quadrant)
+        nc.sync.dma_start(idx4[:], offs4)
+        nc.sync.dma_start(idx[:], offs)
+        nc.sync.dma_start(idx3[:], offs3)
+        nc.sync.dma_start(idx5[:], offs5)
+
+        for zeros in (f2, f1, f3):
+            nc.vector.memset(zeros[:], 0.0)
+
+        states_bf = sb.tile([P, Q, PACK], BF16, name="states_bf", align_bytes=64)
+        nc.vector.tensor_copy(out=states_bf[:], in_=states_raw[:].rearrange("p t q -> p q t"))
+        states_codes = sb.tile([P, Q], U32, name="states_codes", align_bytes=64)
+        states_plane = sb.tile([P, Q], U8, name="states_plane", align_bytes=64)
+        nc.vector.quantize_mx(
+            out=states_codes[:].bitcast(FP8X4), scales=states_plane[:],
+            in_=states_bf[:].rearrange("p q t -> p (q t)"),
+        )
+
+        wq_dealt = sb.tile([P, PACK, P], U32, name="wq_dealt", align_bytes=64)
+        wq_plane_dealt = sb.tile([P, PACK, P], U8, name="wq_plane_dealt", align_bytes=64)
+        nc.scalar.copy(out=wq_dealt[:], in_=wq_codes[:].rearrange("p (m t) -> p t m", t=PACK))
+        nc.vector.tensor_copy(out=wq_plane_dealt[:], in_=wq_plane[:].rearrange("p (m t) -> p t m", t=PACK))
+
+        b_banks = [ps.tile([P, BANK], F32, name="b_bank%d" % j) for j in range(U // BANK)]
+        for j in range(U // BANK):
+            nc.tensor.matmul_mx(
+                out=b_banks[j][:],
+                lhsT=states_codes[:].bitcast(FP8X4), lhsT_scale=states_plane[:],
+                rhs=notes_codes[:, 2 * BANK * j : 2 * BANK * (j + 1)].bitcast(FP4X4),
+                rhs_scale=notes_plane[:, BANK * j : BANK * (j + 1)],
+                start=True, stop=True,
+            )
+        qv_bank = ps.tile([P, PACK, Q], F32, name="qv_bank")
+        for t in range(PACK):
+            nc.tensor.matmul_mx(
+                out=qv_bank[:, t, :],
+                lhsT=wq_dealt[:, t, :].bitcast(FP8X4), lhsT_scale=wq_plane_dealt[:, t, :],
+                rhs=states_codes[:].bitcast(FP8X4), rhs_scale=states_plane[:],
+                start=True, stop=True,
+            )
+
+        b = sb.tile([P, U], F32, name="b")
+        nc.scalar.copy(out=b[:, 0:BANK], in_=b_banks[0][:])
+        nc.vector.tensor_copy(out=b[:, BANK:U], in_=b_banks[1][:])
+
+        qv_bf = sb.tile([P, Q, PACK], BF16, name="qv_bf", align_bytes=64)
+        nc.vector.tensor_copy(out=qv_bf[:], in_=qv_bank[:].rearrange("p t q -> p q t"))
+        qv_codes = sb.tile([P, Q], U32, name="qv_codes", align_bytes=64)
+        qv_plane = sb.tile([P, Q], U8, name="qv_plane", align_bytes=64)
+        nc.vector.quantize_mx(
+            out=qv_codes[:].bitcast(FP8X4), scales=qv_plane[:],
+            in_=qv_bf[:].rearrange("p q t -> p (q t)"),
+        )
+
+        b_picked = [sb.tile([P, HALF], F32, name="b_picked%d" % h) for h in range(2)]
+        for h in range(2):
+            nc.scalar.activation(b_picked[h][:], b[:].indirect(half(idx2, h)), COPY)
+
+        a_banks = [ps.tile([P, BANK], F32, name="a_bank%d" % j) for j in range(T // BANK)]
+        a = sb.tile([P, T], F32, name="a")
+        for j in range(T // BANK):
+            cols = slice(BANK * j, BANK * (j + 1))
+            nc.tensor.matmul_mx(
+                out=a_banks[j][:],
+                lhsT=qv_codes[:].bitcast(FP8X4), lhsT_scale=qv_plane[:],
+                rhs=keys_codes[:, cols].bitcast(FP8X4), rhs_scale=keys_plane[:, cols],
+                start=True, stop=True,
+            )
+            nc.scalar.copy(out=a[:, cols], in_=a_banks[j][:])
+
+        for h in range(2):
+            nc.vector.tensor_copy(f2[:].indirect(half(idx4, h)), b_picked[h][:])
+
+        a_picked = [sb.tile([P, HALF], F32, name="a_picked%d" % h) for h in range(2)]
+        for h in range(2):
+            nc.scalar.activation(a_picked[h][:], a[:].indirect(half(idx, h)), COPY)
+        for h in range(2):
+            nc.vector.tensor_copy(f1[:].indirect(half(idx3, h)), a_picked[h][:])
+
+        m1 = sb.tile([P, Z], F32, name="m1")
+        nc.vector.tensor_tensor(m1[:], f1[:], f2[:], MAX)
+
+        at4 = [sb.tile([P, HALF], F32, name="at4_%d" % h) for h in range(2)]
+        minus_at3 = [sb.tile([P, HALF], F32, name="minus_at3_%d" % h) for h in range(2)]
+        nc.vector.tensor_scalar(minus_at3[0][:], m1[:].indirect(half(idx3, 0)), -1.0, 0.0, MULT, ADD)
+        for h in range(2):
+            nc.scalar.activation(at4[h][:], m1[:].indirect(half(idx4, h)), COPY)
+        nc.scalar.activation(minus_at3[1][:], m1[:].indirect(half(idx3, 1)), COPY, scale=-1.0)
+        for h in range(2):
+            nc.vector.tensor_tensor(f3[:].indirect(half(idx5, h)), at4[h][:], minus_at3[h][:], ADD)
+
+        aa = sb.tile([P, T], F32, name="aa")
+        nc.vector.tensor_tensor(aa[:], a[:], f3[:], ADD)
+
+        result = [sb.tile([P, HALF], F32, name="result%d" % h) for h in range(2)]
+        nc.vector.tensor_copy(result[0][:], aa[:].indirect(half(idx, 0)))
+        nc.scalar.activation(result[1][:], aa[:].indirect(half(idx, 1)), COPY)
+        nc.sync.dma_start(out=out[:, slots(0)], in_=result[0][:])
+        nc.scalar.dma_start(out=out[:, slots(1)], in_=result[1][:])

@@ -21,6 +21,7 @@ COPY = mybir.ActivationFunctionType.Copy
 P = 128
 PACK = 4
 BANK = 512
+A_PIECE = 256
 HALF = I // 2
 LIST_ROWS = 16
 
@@ -65,34 +66,34 @@ def tile_attend_meetinghall_madeside_kernel(
 
         states_raw = sb.tile([P, PACK, Q], F32, name="states_raw")
         notes_codes = sb.tile([P, 2 * U], U8, name="notes_codes", align_bytes=64)
-        wq_codes = sb.tile([P, K], U32, name="wq_codes", align_bytes=64)
+        wq_codes = sb.tile([P, K], U32, name="wq_codes", tag="wq_codes_then_plane", align_bytes=64)
         keys_codes = sb.tile([P, T], U32, name="keys_codes", align_bytes=64)
 
         nc.sync.dma_start(out=states_raw[:], in_=states.rearrange("(p t) q -> p t q", t=PACK))
-        nc.scalar.dma_start(out=notes_codes[:].bitcast(I32), in_=notes_words[0].bitcast(I32))
-        for quadrant in range(4):
-            load_scale_rows(nc.sync, notes_plane, notes_scales, quadrant)
-        nc.scalar.dma_start(
+        load_scale_rows(nc.sync, notes_plane, notes_scales, 0)
+        for quadrant in range(1, 4):
+            load_scale_rows(nc.scalar, notes_plane, notes_scales, quadrant)
+        nc.sync.dma_start(out=notes_codes[:].bitcast(I32), in_=notes_words[0].bitcast(I32))
+        nc.sync.dma_start(
             out=wq_codes[:].bitcast(I32), in_=wq_words[0].rearrange("p k t -> p (k t)").bitcast(I32)
         )
-        load_scale_rows(nc.sync, wq_plane, wq_scales, 0)
-        for quadrant in range(1, 4):
-            load_scale_rows(nc.gpsimd, wq_plane, wq_scales, quadrant)
+        for quadrant in range(4):
+            load_scale_rows(nc.sync if quadrant < 2 else nc.scalar, wq_plane, wq_scales, quadrant)
         nc.sync.dma_start(idx2[:], offs2)
+        nc.sync.dma_start(idx4[:], offs4)
         nc.sync.dma_start(
             out=keys_codes[:].bitcast(I32), in_=keys_words[0].rearrange("p n t -> p (n t)").bitcast(I32)
         )
         for quadrant in range(4):
             load_scale_rows(nc.sync, keys_plane, keys_scales, quadrant)
-        nc.sync.dma_start(idx4[:], offs4)
         nc.sync.dma_start(idx[:], offs)
         nc.sync.dma_start(idx3[:], offs3)
         nc.sync.dma_start(idx5[:], offs5)
 
         for zeros in (f2, f1, f3):
-            nc.vector.memset(zeros[:], 0.0)
+            nc.vector.memset(zeros[:].bitcast(I32), 0)
 
-        states_bf = sb.tile([P, Q, PACK], BF16, name="states_bf", align_bytes=64)
+        states_bf = sb.tile([P, Q, PACK], BF16, name="states_bf", tag="wq_dealt_then_b_picked", align_bytes=64)
         nc.vector.tensor_copy(out=states_bf[:], in_=states_raw[:].rearrange("p t q -> p q t"))
         states_codes = sb.tile([P, Q], U32, name="states_codes", align_bytes=64)
         states_plane = sb.tile([P, Q], U8, name="states_plane", align_bytes=64)
@@ -101,18 +102,21 @@ def tile_attend_meetinghall_madeside_kernel(
             in_=states_bf[:].rearrange("p q t -> p (q t)"),
         )
 
-        wq_dealt = sb.tile([P, PACK, P], U32, name="wq_dealt", align_bytes=64)
-        wq_plane_dealt = sb.tile([P, PACK, P], U8, name="wq_plane_dealt", align_bytes=64)
-        nc.scalar.copy(out=wq_dealt[:], in_=wq_codes[:].rearrange("p (m t) -> p t m", t=PACK))
+        wq_dealt = sb.tile([P, PACK, P], U32, name="wq_dealt", tag="wq_dealt_then_b_picked", align_bytes=64)
+        wq_plane_dealt = sb.tile([P, PACK, P], U8, name="wq_plane_dealt", tag="wq_codes_then_plane", align_bytes=64)
+        nc.vector.tensor_copy(
+            out=wq_dealt[:].bitcast(I32), in_=wq_codes[:].bitcast(I32).rearrange("p (m t) -> p t m", t=PACK)
+        )
         nc.vector.tensor_copy(out=wq_plane_dealt[:], in_=wq_plane[:].rearrange("p (m t) -> p t m", t=PACK))
 
-        b_banks = [ps.tile([P, BANK], F32, name="b_bank%d" % j) for j in range(U // BANK)]
-        for j in range(U // BANK):
+        b_cols = [slice(0, BANK), slice(BANK, U)]
+        b_banks = [ps.tile([P, c.stop - c.start], F32, name="b_bank%d" % c.start) for c in b_cols]
+        for bank, c in zip(b_banks, b_cols):
             nc.tensor.matmul_mx(
-                out=b_banks[j][:],
+                out=bank[:],
                 lhsT=states_codes[:].bitcast(FP8X4), lhsT_scale=states_plane[:],
-                rhs=notes_codes[:, 2 * BANK * j : 2 * BANK * (j + 1)].bitcast(FP4X4),
-                rhs_scale=notes_plane[:, BANK * j : BANK * (j + 1)],
+                rhs=notes_codes[:, 2 * c.start : 2 * c.stop].bitcast(FP4X4),
+                rhs_scale=notes_plane[:, c],
                 start=True, stop=True,
             )
         qv_bank = ps.tile([P, PACK, Q], F32, name="qv_bank")
@@ -125,8 +129,8 @@ def tile_attend_meetinghall_madeside_kernel(
             )
 
         b = sb.tile([P, U], F32, name="b")
-        nc.scalar.copy(out=b[:, 0:BANK], in_=b_banks[0][:])
-        nc.vector.tensor_copy(out=b[:, BANK:U], in_=b_banks[1][:])
+        for bank, c in zip(b_banks, b_cols):
+            nc.scalar.copy(out=b[:, c], in_=bank[:])
 
         qv_bf = sb.tile([P, Q, PACK], BF16, name="qv_bf", align_bytes=64)
         nc.vector.tensor_copy(out=qv_bf[:], in_=qv_bank[:].rearrange("p t q -> p q t"))
@@ -137,14 +141,17 @@ def tile_attend_meetinghall_madeside_kernel(
             in_=qv_bf[:].rearrange("p q t -> p (q t)"),
         )
 
-        b_picked = [sb.tile([P, HALF], F32, name="b_picked%d" % h) for h in range(2)]
+        b_picked = [
+            sb.tile([P, HALF], F32, name="b_picked0", tag="wq_dealt_then_b_picked", align_bytes=64),
+            sb.tile([P, HALF], F32, name="b_picked1"),
+        ]
         for h in range(2):
             nc.scalar.activation(b_picked[h][:], b[:].indirect(half(idx2, h)), COPY)
 
-        a_banks = [ps.tile([P, BANK], F32, name="a_bank%d" % j) for j in range(T // BANK)]
+        a_banks = [ps.tile([P, A_PIECE], F32, name="a_bank%d" % j) for j in range(T // A_PIECE)]
         a = sb.tile([P, T], F32, name="a")
-        for j in range(T // BANK):
-            cols = slice(BANK * j, BANK * (j + 1))
+        for j in range(T // A_PIECE):
+            cols = slice(A_PIECE * j, A_PIECE * (j + 1))
             nc.tensor.matmul_mx(
                 out=a_banks[j][:],
                 lhsT=qv_codes[:].bitcast(FP8X4), lhsT_scale=qv_plane[:],
@@ -156,11 +163,9 @@ def tile_attend_meetinghall_madeside_kernel(
         for h in range(2):
             nc.vector.tensor_copy(f2[:].indirect(half(idx4, h)), b_picked[h][:])
 
-        a_picked = [sb.tile([P, HALF], F32, name="a_picked%d" % h) for h in range(2)]
-        for h in range(2):
-            nc.scalar.activation(a_picked[h][:], a[:].indirect(half(idx, h)), COPY)
-        for h in range(2):
-            nc.vector.tensor_copy(f1[:].indirect(half(idx3, h)), a_picked[h][:])
+        a_picked = sb.tile([P, I], F32, name="a_picked")
+        nc.scalar.activation(a_picked[:], a[:].indirect(idx[:]), COPY)
+        nc.vector.tensor_copy(f1[:].indirect(idx3[:]), a_picked[:])
 
         m1 = sb.tile([P, Z], F32, name="m1")
         nc.vector.tensor_tensor(m1[:], f1[:], f2[:], MAX)

@@ -56,13 +56,12 @@ def tile_attend_meetinghall_madeside_kernel(
         idx5 = sb.tile([P, I // LIST_ROWS], U16, name="idx5")
 
         notes_plane = sb.tile([P, U], U8, name="notes_plane", align_bytes=64)
-        wq_plane = sb.tile([P, K], U8, name="wq_plane", align_bytes=64)
+        wq_plane = sb.tile([P, K], U8, name="wq_plane", tag="wq_plane_then_f3", align_bytes=64)
         keys_plane = sb.tile([P, T], U8, name="keys_plane", align_bytes=64)
         for plane in (notes_plane, wq_plane, keys_plane):
             nc.vector.memset(plane[:].bitcast(I32), 0)
         f1 = sb.tile([P, Z], F32, name="f1")
         f2 = sb.tile([P, Z], F32, name="f2")
-        f3 = sb.tile([P, T], F32, name="f3")
 
         states_raw = sb.tile([P, PACK, Q], F32, name="states_raw")
         notes_codes = sb.tile([P, 2 * U], U8, name="notes_codes", align_bytes=64)
@@ -78,19 +77,21 @@ def tile_attend_meetinghall_madeside_kernel(
             out=wq_codes[:].bitcast(I32), in_=wq_words[0].rearrange("p k t -> p (k t)").bitcast(I32)
         )
         for quadrant in range(4):
-            load_scale_rows(nc.sync if quadrant < 2 else nc.scalar, wq_plane, wq_scales, quadrant)
+            load_scale_rows(nc.scalar if quadrant == 3 else nc.sync, wq_plane, wq_scales, quadrant)
         nc.sync.dma_start(idx2[:], offs2)
-        nc.sync.dma_start(idx4[:], offs4)
         nc.sync.dma_start(
             out=keys_codes[:].bitcast(I32), in_=keys_words[0].rearrange("p n t -> p (n t)").bitcast(I32)
         )
-        for quadrant in range(4):
+        for quadrant in range(2):
+            load_scale_rows(nc.sync, keys_plane, keys_scales, quadrant)
+        nc.sync.dma_start(idx4[:], offs4)
+        for quadrant in range(2, 4):
             load_scale_rows(nc.sync, keys_plane, keys_scales, quadrant)
         nc.sync.dma_start(idx[:], offs)
         nc.sync.dma_start(idx3[:], offs3)
         nc.sync.dma_start(idx5[:], offs5)
 
-        for zeros in (f2, f1, f3):
+        for zeros in (f2, f1):
             nc.vector.memset(zeros[:].bitcast(I32), 0)
 
         states_bf = sb.tile([P, Q, PACK], BF16, name="states_bf", tag="wq_dealt_then_b_picked", align_bytes=64)
@@ -108,6 +109,9 @@ def tile_attend_meetinghall_madeside_kernel(
             out=wq_dealt[:].bitcast(I32), in_=wq_codes[:].bitcast(I32).rearrange("p (m t) -> p t m", t=PACK)
         )
         nc.vector.tensor_copy(out=wq_plane_dealt[:], in_=wq_plane[:].rearrange("p (m t) -> p t m", t=PACK))
+
+        f3 = sb.tile([P, T], F32, name="f3", tag="wq_plane_then_f3", align_bytes=64)
+        nc.vector.memset(f3[:].bitcast(I32), 0)
 
         b_cols = [slice(0, BANK), slice(BANK, U)]
         b_banks = [ps.tile([P, c.stop - c.start], F32, name="b_bank%d" % c.start) for c in b_cols]
@@ -180,7 +184,11 @@ def tile_attend_meetinghall_madeside_kernel(
             nc.vector.tensor_tensor(f3[:].indirect(half(idx5, h)), at4[h][:], minus_at3[h][:], ADD)
 
         aa = sb.tile([P, T], F32, name="aa")
-        nc.vector.tensor_tensor(aa[:], a[:], f3[:], ADD)
+        for j in range(T // A_PIECE - 1):
+            cols = slice(A_PIECE * j, A_PIECE * (j + 1))
+            nc.vector.tensor_tensor(aa[:, cols], a_banks[j][:], f3[:, cols], ADD)
+        cols = slice(T - A_PIECE, T)
+        nc.gpsimd.tensor_tensor(aa[:, cols], a[:, cols], f3[:, cols], ADD)
 
         result = [sb.tile([P, HALF], F32, name="result%d" % h) for h in range(2)]
         nc.vector.tensor_copy(result[0][:], aa[:].indirect(half(idx, 0)))

@@ -56,12 +56,13 @@ def tile_attend_meetinghall_madeside_kernel(
         idx5 = sb.tile([P, I // LIST_ROWS], U16, name="idx5")
 
         notes_plane = sb.tile([P, U], U8, name="notes_plane", align_bytes=64)
-        wq_plane = sb.tile([P, K], U8, name="wq_plane", tag="wq_plane_then_f3", align_bytes=64)
+        wq_plane = sb.tile([P, K], U8, name="wq_plane", align_bytes=64)
         keys_plane = sb.tile([P, T], U8, name="keys_plane", align_bytes=64)
         for plane in (notes_plane, wq_plane, keys_plane):
             nc.vector.memset(plane[:].bitcast(I32), 0)
         f1 = sb.tile([P, Z], F32, name="f1")
         f2 = sb.tile([P, Z], F32, name="f2")
+        f3 = sb.tile([P, T], F32, name="f3")
 
         states_raw = sb.tile([P, PACK, Q], F32, name="states_raw")
         notes_codes = sb.tile([P, 2 * U], U8, name="notes_codes", align_bytes=64)
@@ -69,9 +70,8 @@ def tile_attend_meetinghall_madeside_kernel(
         keys_codes = sb.tile([P, T], U32, name="keys_codes", align_bytes=64)
 
         nc.sync.dma_start(out=states_raw[:], in_=states.rearrange("(p t) q -> p t q", t=PACK))
-        load_scale_rows(nc.sync, notes_plane, notes_scales, 0)
-        for quadrant in range(1, 4):
-            load_scale_rows(nc.scalar, notes_plane, notes_scales, quadrant)
+        for quadrant in range(4):
+            load_scale_rows(nc.sync if quadrant < 2 else nc.scalar, notes_plane, notes_scales, quadrant)
         nc.sync.dma_start(out=notes_codes[:].bitcast(I32), in_=notes_words[0].bitcast(I32))
         nc.sync.dma_start(
             out=wq_codes[:].bitcast(I32), in_=wq_words[0].rearrange("p k t -> p (k t)").bitcast(I32)
@@ -91,10 +91,10 @@ def tile_attend_meetinghall_madeside_kernel(
         nc.sync.dma_start(idx3[:], offs3)
         nc.sync.dma_start(idx5[:], offs5)
 
-        for zeros in (f2, f1):
+        for zeros in (f2, f1, f3):
             nc.vector.memset(zeros[:].bitcast(I32), 0)
 
-        states_bf = sb.tile([P, Q, PACK], BF16, name="states_bf", tag="wq_dealt_then_b_picked", align_bytes=64)
+        states_bf = sb.tile([P, Q, PACK], BF16, name="states_bf", tag="states_bf_then_wq_dealt", align_bytes=64)
         nc.vector.tensor_copy(out=states_bf[:], in_=states_raw[:].rearrange("p t q -> p q t"))
         states_codes = sb.tile([P, Q], U32, name="states_codes", align_bytes=64)
         states_plane = sb.tile([P, Q], U8, name="states_plane", align_bytes=64)
@@ -103,15 +103,15 @@ def tile_attend_meetinghall_madeside_kernel(
             in_=states_bf[:].rearrange("p q t -> p (q t)"),
         )
 
-        wq_dealt = sb.tile([P, PACK, P], U32, name="wq_dealt", tag="wq_dealt_then_b_picked", align_bytes=64)
+        wq_dealt = sb.tile([P, PACK, P], U32, name="wq_dealt", tag="states_bf_then_wq_dealt", align_bytes=64)
         wq_plane_dealt = sb.tile([P, PACK, P], U8, name="wq_plane_dealt", tag="wq_codes_then_plane", align_bytes=64)
         nc.vector.tensor_copy(
             out=wq_dealt[:].bitcast(I32), in_=wq_codes[:].bitcast(I32).rearrange("p (m t) -> p t m", t=PACK)
         )
-        nc.vector.tensor_copy(out=wq_plane_dealt[:], in_=wq_plane[:].rearrange("p (m t) -> p t m", t=PACK))
-
-        f3 = sb.tile([P, T], F32, name="f3", tag="wq_plane_then_f3", align_bytes=64)
-        nc.vector.memset(f3[:].bitcast(I32), 0)
+        for t in range(PACK):
+            nc.vector.tensor_copy(
+                out=wq_plane_dealt[:, t, :], in_=wq_plane[:].rearrange("p (m t) -> p t m", t=PACK)[:, t, :]
+            )
 
         b_cols = [slice(0, BANK), slice(BANK, U)]
         b_banks = [ps.tile([P, c.stop - c.start], F32, name="b_bank%d" % c.start) for c in b_cols]
@@ -137,18 +137,18 @@ def tile_attend_meetinghall_madeside_kernel(
             nc.scalar.copy(out=b[:, c], in_=bank[:])
 
         qv_bf = sb.tile([P, Q, PACK], BF16, name="qv_bf", align_bytes=64)
-        nc.vector.tensor_copy(out=qv_bf[:], in_=qv_bank[:].rearrange("p t q -> p q t"))
+        q_halves = [slice(0, Q // 2), slice(Q // 2, Q)]
+        for rows in q_halves:
+            nc.vector.tensor_copy(out=qv_bf[:, rows, :], in_=qv_bank[:, :, rows].rearrange("p t q -> p q t"))
         qv_codes = sb.tile([P, Q], U32, name="qv_codes", align_bytes=64)
         qv_plane = sb.tile([P, Q], U8, name="qv_plane", align_bytes=64)
-        nc.vector.quantize_mx(
-            out=qv_codes[:].bitcast(FP8X4), scales=qv_plane[:],
-            in_=qv_bf[:].rearrange("p q t -> p (q t)"),
-        )
+        for rows in q_halves:
+            nc.vector.quantize_mx(
+                out=qv_codes[:, rows].bitcast(FP8X4), scales=qv_plane[:, rows],
+                in_=qv_bf[:, rows, :].rearrange("p q t -> p (q t)"),
+            )
 
-        b_picked = [
-            sb.tile([P, HALF], F32, name="b_picked0", tag="wq_dealt_then_b_picked", align_bytes=64),
-            sb.tile([P, HALF], F32, name="b_picked1"),
-        ]
+        b_picked = [sb.tile([P, HALF], F32, name="b_picked%d" % h) for h in range(2)]
         for h in range(2):
             nc.scalar.activation(b_picked[h][:], b[:].indirect(half(idx2, h)), COPY)
 

from contextlib import ExitStack

import concourse.mybir as mybir

D, K, T, U, Z, I, Q = 512, 512, 1024, 1024, 1024, 512, 128
FLOPS = 2 * Q * (D * K + K * T + D * U)

F32 = mybir.dt.float32
BF16 = mybir.dt.bfloat16
I32 = mybir.dt.int32
U32 = mybir.dt.uint32
U16 = mybir.dt.uint16
U8 = mybir.dt.uint8
FP8X4 = mybir.dt.float8_e4m3fn_x4
FP4X4 = mybir.dt.float4_e2m1fn_x4
ADD = mybir.AluOpType.add
MULT = mybir.AluOpType.mult
MAX = mybir.AluOpType.max
COPY = mybir.ActivationFunctionType.Copy

P = 128
PACK = 4
BANK = 512
A_PIECE = 256
HALF = I // 2
LIST_ROWS = 16


def load_scale_rows(queue, plane, scales, quadrant):
    queue.dma_start(
        out=plane[32 * quadrant : 32 * quadrant + 4, :].bitcast(I32),
        in_=scales[0, 4 * quadrant : 4 * quadrant + 4, :].bitcast(I32),
    )


def tile_attend_meetinghall_madeside_kernel(
    tc, states, wq_words, wq_scales, keys_words, keys_scales, notes_words, notes_scales,
    offs, offs2, offs3, offs4, offs5, out,
):
    nc = tc.nc
    with ExitStack() as ctx:
        sb = ctx.enter_context(tc.tile_pool(name="sb", bufs=1))
        ps = ctx.enter_context(tc.psum_pool(name="ps", bufs=1))

        def half(lists, h):
            cols = HALF // LIST_ROWS
            return lists[:, h * cols : (h + 1) * cols]

        def slots(h):
            return slice(h * HALF, (h + 1) * HALF)

        idx = sb.tile([P, I // LIST_ROWS], U16, name="idx")
        idx2 = sb.tile([P, I // LIST_ROWS], U16, name="idx2")
        idx3 = sb.tile([P, I // LIST_ROWS], U16, name="idx3")
        idx4 = sb.tile([P, I // LIST_ROWS], U16, name="idx4")
        idx5 = sb.tile([P, I // LIST_ROWS], U16, name="idx5")

        notes_plane = sb.tile([P, U], U8, name="notes_plane", align_bytes=64)
        wq_plane = sb.tile([P, K], U8, name="wq_plane", align_bytes=64)
        keys_plane = sb.tile([P, T], U8, name="keys_plane", align_bytes=64)
        for plane in (notes_plane, wq_plane, keys_plane):
            nc.vector.memset(plane[:].bitcast(I32), 0)
        f1 = sb.tile([P, Z], F32, name="f1")
        f2 = sb.tile([P, Z], F32, name="f2")
        f3 = sb.tile([P, T], F32, name="f3")

        states_raw = sb.tile([P, PACK, Q], F32, name="states_raw")
        notes_codes = sb.tile([P, 2 * U], U8, name="notes_codes", align_bytes=64)
        wq_codes = sb.tile([P, K], U32, name="wq_codes", tag="wq_codes_then_plane", align_bytes=64)
        keys_codes = sb.tile([P, T], U32, name="keys_codes", align_bytes=64)

        nc.sync.dma_start(out=states_raw[:], in_=states.rearrange("(p t) q -> p t q", t=PACK))
        for quadrant in range(4):
            load_scale_rows(nc.sync if quadrant < 2 else nc.scalar, notes_plane, notes_scales, quadrant)
        nc.sync.dma_start(out=notes_codes[:].bitcast(I32), in_=notes_words[0].bitcast(I32))
        nc.sync.dma_start(
            out=wq_codes[:].bitcast(I32), in_=wq_words[0].rearrange("p k t -> p (k t)").bitcast(I32)
        )
        for quadrant in range(4):
            load_scale_rows(nc.scalar if quadrant == 3 else nc.sync, wq_plane, wq_scales, quadrant)
        nc.sync.dma_start(idx2[:], offs2)
        nc.sync.dma_start(
            out=keys_codes[:].bitcast(I32), in_=keys_words[0].rearrange("p n t -> p (n t)").bitcast(I32)
        )
        for quadrant in range(2):
            load_scale_rows(nc.sync, keys_plane, keys_scales, quadrant)
        nc.sync.dma_start(idx4[:], offs4)
        for quadrant in range(2, 4):
            load_scale_rows(nc.sync, keys_plane, keys_scales, quadrant)
        nc.sync.dma_start(idx[:], offs)
        nc.sync.dma_start(idx3[:], offs3)
        nc.sync.dma_start(idx5[:], offs5)

        for zeros in (f2, f1, f3):
            nc.vector.memset(zeros[:].bitcast(I32), 0)

        states_bf = sb.tile([P, Q, PACK], BF16, name="states_bf", tag="states_bf_then_wq_dealt", align_bytes=64)
        nc.vector.tensor_copy(out=states_bf[:], in_=states_raw[:].rearrange("p t q -> p q t"))
        states_codes = sb.tile([P, Q], U32, name="states_codes", align_bytes=64)
        states_plane = sb.tile([P, Q], U8, name="states_plane", align_bytes=64)
        nc.vector.quantize_mx(
            out=states_codes[:].bitcast(FP8X4), scales=states_plane[:],
            in_=states_bf[:].rearrange("p q t -> p (q t)"),
        )

        wq_dealt = sb.tile([P, PACK, P], U32, name="wq_dealt", tag="states_bf_then_wq_dealt", align_bytes=64)
        wq_plane_dealt = sb.tile([P, PACK, P], U8, name="wq_plane_dealt", tag="wq_codes_then_plane", align_bytes=64)
        nc.vector.tensor_copy(
            out=wq_dealt[:].bitcast(I32), in_=wq_codes[:].bitcast(I32).rearrange("p (m t) -> p t m", t=PACK)
        )
        for t in range(PACK):
            nc.vector.tensor_copy(
                out=wq_plane_dealt[:, t, :], in_=wq_plane[:].rearrange("p (m t) -> p t m", t=PACK)[:, t, :]
            )

        b_cols = [slice(0, BANK), slice(BANK, U)]
        b_banks = [ps.tile([P, c.stop - c.start], F32, name="b_bank%d" % c.start) for c in b_cols]
        for bank, c in zip(b_banks, b_cols):
            nc.tensor.matmul_mx(
                out=bank[:],
                lhsT=states_codes[:].bitcast(FP8X4), lhsT_scale=states_plane[:],
                rhs=notes_codes[:, 2 * c.start : 2 * c.stop].bitcast(FP4X4),
                rhs_scale=notes_plane[:, c],
                start=True, stop=True,
            )
        qv_bank = ps.tile([P, PACK, Q], F32, name="qv_bank")
        for t in range(PACK):
            nc.tensor.matmul_mx(
                out=qv_bank[:, t, :],
                lhsT=wq_dealt[:, t, :].bitcast(FP8X4), lhsT_scale=wq_plane_dealt[:, t, :],
                rhs=states_codes[:].bitcast(FP8X4), rhs_scale=states_plane[:],
                start=True, stop=True,
            )

        b = sb.tile([P, U], F32, name="b")
        for bank, c in zip(b_banks, b_cols):
            nc.scalar.copy(out=b[:, c], in_=bank[:])

        qv_bf = sb.tile([P, Q, PACK], BF16, name="qv_bf", align_bytes=64)
        q_halves = [slice(0, Q // 2), slice(Q // 2, Q)]
        for rows in q_halves:
            nc.vector.tensor_copy(out=qv_bf[:, rows, :], in_=qv_bank[:, :, rows].rearrange("p t q -> p q t"))
        qv_codes = sb.tile([P, Q], U32, name="qv_codes", align_bytes=64)
        qv_plane = sb.tile([P, Q], U8, name="qv_plane", align_bytes=64)
        for rows in q_halves:
            nc.vector.quantize_mx(
                out=qv_codes[:, rows].bitcast(FP8X4), scales=qv_plane[:, rows],
                in_=qv_bf[:, rows, :].rearrange("p q t -> p (q t)"),
            )

        b_picked = [sb.tile([P, HALF], F32, name="b_picked%d" % h) for h in range(2)]
        for h in range(2):
            nc.scalar.activation(b_picked[h][:], b[:].indirect(half(idx2, h)), COPY)

        a_banks = [ps.tile([P, A_PIECE], F32, name="a_bank%d" % j) for j in range(T // A_PIECE)]
        a = sb.tile([P, T], F32, name="a")
        for j in range(T // A_PIECE):
            cols = slice(A_PIECE * j, A_PIECE * (j + 1))
            nc.tensor.matmul_mx(
                out=a_banks[j][:],
                lhsT=qv_codes[:].bitcast(FP8X4), lhsT_scale=qv_plane[:],
                rhs=keys_codes[:, cols].bitcast(FP8X4), rhs_scale=keys_plane[:, cols],
                start=True, stop=True,
            )
            nc.scalar.copy(out=a[:, cols], in_=a_banks[j][:])

        for h in range(2):
            nc.vector.tensor_copy(f2[:].indirect(half(idx4, h)), b_picked[h][:])

        a_picked = sb.tile([P, I], F32, name="a_picked")
        nc.scalar.activation(a_picked[:], a[:].indirect(idx[:]), COPY)
        nc.vector.tensor_copy(f1[:].indirect(idx3[:]), a_picked[:])

        m1 = sb.tile([P, Z], F32, name="m1")
        nc.vector.tensor_tensor(m1[:], f1[:], f2[:], MAX)

        at4 = [sb.tile([P, HALF], F32, name="at4_%d" % h) for h in range(2)]
        minus_at3 = [sb.tile([P, HALF], F32, name="minus_at3_%d" % h) for h in range(2)]
        nc.vector.tensor_scalar(minus_at3[0][:], m1[:].indirect(half(idx3, 0)), -1.0, 0.0, MULT, ADD)
        for h in range(2):
            nc.scalar.activation(at4[h][:], m1[:].indirect(half(idx4, h)), COPY)
        nc.scalar.activation(minus_at3[1][:], m1[:].indirect(half(idx3, 1)), COPY, scale=-1.0)
        for h in range(2):
            nc.vector.tensor_tensor(f3[:].indirect(half(idx5, h)), at4[h][:], minus_at3[h][:], ADD)

        aa = sb.tile([P, T], F32, name="aa")
        for j in range(T // A_PIECE - 1):
            cols = slice(A_PIECE * j, A_PIECE * (j + 1))
            nc.vector.tensor_tensor(aa[:, cols], a_banks[j][:], f3[:, cols], ADD)
        cols = slice(T - A_PIECE, T)
        nc.gpsimd.tensor_tensor(aa[:, cols], a[:, cols], f3[:, cols], ADD)

        result = [sb.tile([P, HALF], F32, name="result%d" % h) for h in range(2)]
        nc.vector.tensor_copy(result[0][:], aa[:].indirect(half(idx, 0)))
        nc.scalar.activation(result[1][:], aa[:].indirect(half(idx, 1)), COPY)
        nc.sync.dma_start(out=out[:, slots(0)], in_=result[0][:])
        nc.scalar.dma_start(out=out[:, slots(1)], in_=result[1][:])
